import numpy as np, ml_dtypes
CORES = [9,13,81,85,89,93,97,101,113,117,121,125]
N = 12
WB, KB, QP = 4, 1, 64
def setup_inputs(rng):
    return {"q": rng.standard_normal((N, 128, QP), dtype=np.float32).astype(ml_dtypes.bfloat16), "k": rng.standard_normal((N, 128, KB * 128), dtype=np.float32).astype(ml_dtypes.bfloat16), "v": rng.standard_normal((N, 128, KB * 128), dtype=np.float32).astype(ml_dtypes.bfloat16)}
def setup_inputs_big(rng):
    d = setup_inputs(rng)
    for k in ("q", "k", "v"): d[k] = (d[k].astype(np.float32) * 1024.0).astype(d[k].dtype)
    return d
def setup_inputs_small(rng):
    d = setup_inputs(rng)
    for k in ("q", "k", "v"): d[k] = (d[k].astype(np.float32) * (1 / 1024.0)).astype(d[k].dtype)
    return d
def setup_inputs_apart(rng):
    d = setup_inputs(rng)
    f = (10.0 ** rng.permutation(np.linspace(-1.5, 1.5, N))).astype(np.float32).reshape(N, 1, 1)
    for k in ("q", "k", "v"): d[k] = (d[k].astype(np.float32) * f).astype(d[k].dtype)
    return d
def reference(q, k, v):
    Q, K, V = q.astype(np.float64), k.astype(np.float64), v.astype(np.float64)
    y = np.zeros((N, 128, QP))
    for r in range(N):
        for j in range(max(0, r - WB), r + 1):
            for b in range(KB):
                S = np.maximum(K[j][:, 128 * b:128 * b + 128].T @ Q[r], 0.0)
                y[r] += V[j][:, 128 * b:128 * b + 128].T @ S
    return {"y": y.astype(ml_dtypes.bfloat16 if q.dtype != np.float64 else np.float64)}

@@ -1,0 +1,239 @@
+from concourse.bass import DstId, RemoteDMATransfer
+from concourse.mybir import AluOpType
+
+WB = 4
+D = 128
+QP = 64
+HAND = 4
+FAR = False
+
+SCRATCH = {
+    "kvd": ("dram", [128, 2 * D], "bfloat16"),
+    "rl": ("dram", [128, 2 * D], "bfloat16"),
+    "kvs": ("sbuf", [128, 2 * D], "bfloat16"),
+    "qs": ("sbuf", [128, QP], "bfloat16"),
+    "land0": ("sbuf", [128, 2 * D], "bfloat16"),
+    "land1": ("sbuf", [128, 2 * D], "bfloat16"),
+    "land2": ("sbuf", [128, 2 * D], "bfloat16"),
+    "land3": ("sbuf", [128, 2 * D], "bfloat16"),
+    "zero": ("sbuf", [128, QP], "float32"),
+    "s0": ("sbuf", [128, QP], "bfloat16"),
+    "s1": ("sbuf", [128, QP], "bfloat16"),
+    "s2": ("sbuf", [128, QP], "bfloat16"),
+    "s3": ("sbuf", [128, QP], "bfloat16"),
+    "s4": ("sbuf", [128, QP], "bfloat16"),
+    "ysb": ("sbuf", [128, QP], "bfloat16"),
+    "ps0": ("psum", [128, 512], "float32"),
+    "ps1": ("psum", [128, 512], "float32"),
+    "ps2": ("psum", [128, 512], "float32"),
+    "ps3": ("psum", [128, 512], "float32"),
+    "ps4": ("psum", [128, 512], "float32"),
+    "po": ("psum", [128, 512], "float32"),
+}
+SEMAPHORES = ["ldd", "lds", "rin", "sent", "arr0", "arr1", "arr2", "arr3", "zs",
+              "sS0", "sS1", "sS2", "sS3", "sS4", "sR0", "sR1", "sR2", "sR3", "sR4", "sO", "sY", "st"]
+
+
+def _bits(m):
+    return [b for b in range(m.bit_length()) if (m >> b) & 1]
+
+
+def _every(topo):
+    return range(topo.CHIPS * topo.CORES_PER_CHIP)
+
+
+def _pick(topo, src, dsts, n, busy):
+    allowed = -1
+    for d in dsts:
+        allowed &= topo.mask(src, d)
+    narrow = -1
+    for x in _every(topo):
+        if x != src:
+            narrow &= topo.mask(src, x)
+    free = [b for b in _bits(allowed) if b not in busy]
+    order = [b for b in free if not (narrow >> b) & 1] + [b for b in free if (narrow >> b) & 1]
+    m = 0
+    for b in order[:n]:
+        m |= 1 << b
+        busy.add(b)
+    return m
+
+
+def _pow2(n, cap):
+    p = 1
+    while p * 2 <= min(n, cap):
+        p *= 2
+    return p
+
+
+def _plan(T, topo):
+    cores = list(T.cores)
+    n = len(cores)
+    group = set(cores)
+    taken = set()
+    plan = []
+    for j, cj in enumerate(cores):
+        dests = list(range(j + 1, min(n, j + WB + 1)))
+        own = [r for r in dests if topo.may_write(cj, cores[r])]
+        near = [r for r in own if topo.chip(cores[r]) == topo.chip(cj)]
+        far = [r for r in own if topo.chip(cores[r]) != topo.chip(cj)]
+        cross = [r for r in dests if r not in own]
+        relays = []
+        if cross:
+            cand = [h for h in _every(topo)
+                    if h not in group and h not in taken
+                    and topo.chip(h) == topo.chip(cj) and topo.die(h) == topo.die(cj)
+                    and all(topo.may_write(h, cores[r]) for r in cross)]
+            if FAR and len(cross) > len(cand):
+                for r in cross[len(cand):]:
+                    there = [h for h in _every(topo)
+                             if h not in group and h not in taken
+                             and topo.mates(topo.chip(h), topo.chip(cores[r]))
+                             and topo.same_plane(topo.chip(h), topo.chip(cj)) and topo.die(h) == topo.die(cj)
+                             and topo.may_write(h, cores[r])]
+                    relays.append((there[0], [r]))
+                    taken.add(there[0])
+                cross = cross[:len(cand)]
+            k = min(len(cand), len(cross))
+            per = -(-len(cross) // k)
+            for i in range(k):
+                part = cross[i * per:(i + 1) * per]
+                if part:
+                    relays.append((cand[i], part))
+                    taken.add(cand[i])
+        plan.append({"near": near, "far": far, "relays": relays})
+    return plan
+
+
+def _width(topo, src, dsts):
+    allowed = -1
+    for d in dsts:
+        allowed &= topo.mask(src, d)
+    return _pow2(len(_bits(allowed)), 8)
+
+
+def _hands(topo, src, relays):
+    out = []
+    for same in (False, True):
+        hs = [h for h, p in relays if (topo.chip(h) == topo.chip(src)) == same]
+        if hs:
+            out.append((hs, _pow2(HAND * len(hs), 8)))
+    return out
+
+
+def _xfer(topo, dsts, mask, sem, src_ap, dst_ap):
+    ids = []
+    for d in dsts:
+        a = topo.addr(d)
+        ids.append(DstId(rid=a[0], pnc=a[1]))
+    return RemoteDMATransfer(dst_ids=ids, dma_engine_mask=mask, remote_sem=sem,
+                             srcs=[src_ap], dsts=[dst_ap] * len(ids), alu_op=0)
+
+
+def _relay_program(g, core, T, topo, j, part, plan):
+    cores = list(T.cores)
+    dsts = [cores[r] for r in part]
+    for hs, hw in _hands(topo, cores[j], plan[j]["relays"]):
+        if core in hs:
+            g.wait_ge(T.sem.rin, hw)
+    w = _width(topo, core, dsts)
+    m = _pick(topo, core, dsts, w, set())
+    g.remote_dma_fused([_xfer(topo, dsts, m, T.sem["arr%d" % (j % WB)], T.rl[:], T["land%d" % (j % WB)][:])],
+                       local_sem=T.sem.sent)
+    g.wait_ge(T.sem.sent, w)
+
+
+def rank_program(g, core, T, topo):
+    plan = _plan(T, topo)
+    cores = list(T.cores)
+    rank = T.rank_of(core)
+    if rank is None:
+        for j, p in enumerate(plan):
+            for h, part in p["relays"]:
+                if h == core:
+                    _relay_program(g, core, T, topo, j, part, plan)
+        return
+
+    me = plan[rank]
+    sends = bool(me["near"] or me["far"] or me["relays"])
+
+    if sends:
+        g.sync.dma_start(T.kvd[:, 0:D], T.k[:]).then_inc(T.sem.ldd, 16)
+        g.scalar.dma_start(T.kvd[:, D:2 * D], T.v[:]).then_inc(T.sem.ldd, 16)
+    g.sync.dma_start(T.kvs[:, 0:D], T.k[:]).then_inc(T.sem.lds, 16)
+    g.scalar.dma_start(T.kvs[:, D:2 * D], T.v[:]).then_inc(T.sem.lds, 16)
+    g.scalar.dma_start(T.qs[:], T.q[:]).then_inc(T.sem.lds, 16)
+    g.vector.memset(T.zero[:], 0.0).then_inc(T.sem.zs, 1)
+
+    if sends:
+        slot = T["land%d" % (rank % WB)][:]
+        sem = T.sem["arr%d" % (rank % WB)]
+        total = 0
+        g.wait_ge(T.sem.ldd, 32)
+        if me["relays"]:
+            busy = set()
+            tr = []
+            for hs, w in _hands(topo, core, me["relays"]):
+                tr.append(_xfer(topo, hs, _pick(topo, core, hs, w, busy), T.sem.rin, T.kvd[:], T.rl[:]))
+                total += w
+            g.remote_dma_fused(tr, local_sem=T.sem.sent)
+        busy = set()
+        tr = []
+        for part in (me["far"], me["near"]):
+            if part:
+                dsts = [cores[r] for r in part]
+                w = _width(topo, core, dsts)
+                tr.append(_xfer(topo, dsts, _pick(topo, core, dsts, w, busy), sem, T.kvd[:], slot))
+                total += w
+        if tr:
+            g.remote_dma_fused(tr, local_sem=T.sem.sent)
+        g.wait_ge(T.sem.sent, total)
+
+    early, late = [], []
+    for j in range(max(0, rank - WB), rank):
+        p = plan[j]
+        if rank in p["near"]:
+            early.append((0, j, _width(topo, cores[j], [cores[r] for r in p["near"]])))
+        elif rank in p["far"]:
+            early.append((1, j, _width(topo, cores[j], [cores[r] for r in p["far"]])))
+        else:
+            for h, part in p["relays"]:
+                if rank in part:
+                    late.append((len(part), j, _width(topo, h, [cores[r] for r in part])))
+    early.sort()
+    late.sort()
+    groups = [[(None, rank, 0)] + early, late]
+    n_src = 1 + len(early) + len(late)
+
+    i = 0
+    for grp in groups:
+        first = i
+        for c, j, w in grp:
+            if j == rank:
+                g.tensor.wait_ge(T.sem.lds, 48)
+                kv = T.kvs
+            else:
+                g.tensor.wait_ge(T.sem["arr%d" % (j % WB)], w)
+                kv = T["land%d" % (j % WB)]
+            g.tensor.matmul(T["ps%d" % i][:, 0:QP], kv[:, 0:D], T.qs[:], True, True).then_inc(T.sem["sS%d" % i], 1)
+            i += 1
+        i = first
+        for c, j, w in grp:
+            kv = T.kvs if j == rank else T["land%d" % (j % WB)]
+            g.tensor.wait_ge(T.sem["sR%d" % i], 1)
+            mm = g.tensor.matmul(T.po[:, 0:QP], kv[:, D:2 * D], T["s%d" % i][:], i == 0, i == n_src - 1)
+            if i == n_src - 1:
+                mm.then_inc(T.sem.sO, 1)
+            i += 1
+
+    g.vector.wait_ge(T.sem.zs, 1)
+    for i in range(n_src):
+        g.vector.wait_ge(T.sem["sS%d" % i], 1)
+        g.vector.tensor_tensor(T["s%d" % i][:], T["ps%d" % i][:, 0:QP], T.zero[:], AluOpType.max).then_inc(
+            T.sem["sR%d" % i], 1)
+    g.vector.wait_ge(T.sem.sO, 1)
+    g.vector.tensor_copy(T.ysb[:], T.po[:, 0:QP]).then_inc(T.sem.sY, 1)
+
+    g.sync.wait_ge(T.sem.sY, 1)
+    g.sync.dma_start(T.y[:], T.ysb[:]).then_inc(T.sem.st, 16)
+    g.sync.wait_ge(T.sem.st, 16)

@@ -5,11 +5,13 @@ WB = 4
 D = 128
 QP = 64
 HAND = 4
-FAR = False
+PIPE = True
 
 SCRATCH = {
-    "kvd": ("dram", [128, 2 * D], "bfloat16"),
-    "rl": ("dram", [128, 2 * D], "bfloat16"),
+    "kd": ("dram", [128, D], "bfloat16"),
+    "vd": ("dram", [128, D], "bfloat16"),
+    "rk": ("dram", [128, D], "bfloat16"),
+    "rv": ("dram", [128, D], "bfloat16"),
     "kvs": ("sbuf", [128, 2 * D], "bfloat16"),
     "qs": ("sbuf", [128, QP], "bfloat16"),
     "land0": ("sbuf", [128, 2 * D], "bfloat16"),
@@ -30,7 +32,8 @@ SCRATCH = {
     "ps4": ("psum", [128, 512], "float32"),
     "po": ("psum", [128, 512], "float32"),
 }
-SEMAPHORES = ["ldd", "lds", "rin", "sent", "arr0", "arr1", "arr2", "arr3", "zs",
+SEMAPHORES = ["ldk", "ldv", "lds", "rink", "rinv", "sent",
+              "ak0", "ak1", "ak2", "ak3", "av0", "av1", "av2", "av3", "zs",
               "sS0", "sS1", "sS2", "sS3", "sS4", "sR0", "sR1", "sR2", "sR3", "sR4", "sO", "sY", "st"]
 
 
@@ -84,16 +87,6 @@ def _plan(T, topo):
                     if h not in group and h not in taken
                     and topo.chip(h) == topo.chip(cj) and topo.die(h) == topo.die(cj)
                     and all(topo.may_write(h, cores[r]) for r in cross)]
-            if FAR and len(cross) > len(cand):
-                for r in cross[len(cand):]:
-                    there = [h for h in _every(topo)
-                             if h not in group and h not in taken
-                             and topo.mates(topo.chip(h), topo.chip(cores[r]))
-                             and topo.same_plane(topo.chip(h), topo.chip(cj)) and topo.die(h) == topo.die(cj)
-                             and topo.may_write(h, cores[r])]
-                    relays.append((there[0], [r]))
-                    taken.add(there[0])
-                cross = cross[:len(cand)]
             k = min(len(cand), len(cross))
             per = -(-len(cross) // k)
             for i in range(k):
@@ -112,15 +105,6 @@ def _width(topo, src, dsts):
     return _pow2(len(_bits(allowed)), 8)
 
 
-def _hands(topo, src, relays):
-    out = []
-    for same in (False, True):
-        hs = [h for h, p in relays if (topo.chip(h) == topo.chip(src)) == same]
-        if hs:
-            out.append((hs, _pow2(HAND * len(hs), 8)))
-    return out
-
-
 def _xfer(topo, dsts, mask, sem, src_ap, dst_ap):
     ids = []
     for d in dsts:
@@ -130,17 +114,55 @@ def _xfer(topo, dsts, mask, sem, src_ap, dst_ap):
                              srcs=[src_ap], dsts=[dst_ap] * len(ids), alu_op=0)
 
 
+def _send(g, T, topo, src, jobs, ahead, waits):
+    total = 0
+    if ahead:
+        masks = []
+        busy = set()
+        for dsts, w, kk, vv in jobs:
+            masks.append(_pick(topo, src, dsts, w, busy))
+        for half in (0, 1):
+            for sem, val in waits[half]:
+                g.wait_ge(sem, val)
+            tr = []
+            for (dsts, w, kk, vv), m in zip(jobs, masks):
+                a = (kk, vv)[half]
+                tr.append(_xfer(topo, dsts, m, a[2], a[0], a[1]))
+                total += w
+            g.remote_dma_fused(tr, local_sem=T.sem.sent)
+    else:
+        for half in (0, 1):
+            for sem, val in waits[half]:
+                g.wait_ge(sem, val)
+        busy = set()
+        tr = []
+        for dsts, w, kk, vv in jobs:
+            for a in (kk, vv):
+                tr.append(_xfer(topo, dsts, _pick(topo, src, dsts, w // 2, busy), a[2], a[0], a[1]))
+                total += w // 2
+        g.remote_dma_fused(tr, local_sem=T.sem.sent)
+    return total
+
+
+def _count(w, ahead):
+    return w if ahead else w // 2
+
+
+def _hand_width(relays):
+    return _pow2(HAND * len(relays), 8)
+
+
 def _relay_program(g, core, T, topo, j, part, plan):
     cores = list(T.cores)
     dsts = [cores[r] for r in part]
-    for hs, hw in _hands(topo, cores[j], plan[j]["relays"]):
-        if core in hs:
-            g.wait_ge(T.sem.rin, hw)
+    hw = _count(_hand_width(plan[j]["relays"]), PIPE)
+    s = j % WB
     w = _width(topo, core, dsts)
-    m = _pick(topo, core, dsts, w, set())
-    g.remote_dma_fused([_xfer(topo, dsts, m, T.sem["arr%d" % (j % WB)], T.rl[:], T["land%d" % (j % WB)][:])],
-                       local_sem=T.sem.sent)
-    g.wait_ge(T.sem.sent, w)
+    total = _send(g, T, topo, core,
+                  [(dsts, w, (T.rk[:], T["land%d" % s][:, 0:D], T.sem["ak%d" % s]),
+                    (T.rv[:], T["land%d" % s][:, D:2 * D], T.sem["av%d" % s]))],
+                  PIPE, ([(T.sem.rink, hw)], [(T.sem.rinv, hw)]))
+    g.wait_ge(T.sem.sent, total)
 
 
 def rank_program(g, core, T, topo):
@@ -158,48 +180,45 @@ def rank_program(g, core, T, topo):
     sends = bool(me["near"] or me["far"] or me["relays"])
 
     if sends:
-        g.sync.dma_start(T.kvd[:, 0:D], T.k[:]).then_inc(T.sem.ldd, 16)
-        g.scalar.dma_start(T.kvd[:, D:2 * D], T.v[:]).then_inc(T.sem.ldd, 16)
+        g.sync.dma_start(T.kd[:], T.k[:]).then_inc(T.sem.ldk, 16)
+        g.scalar.dma_start(T.vd[:], T.v[:]).then_inc(T.sem.ldv, 16)
     g.sync.dma_start(T.kvs[:, 0:D], T.k[:]).then_inc(T.sem.lds, 16)
     g.scalar.dma_start(T.kvs[:, D:2 * D], T.v[:]).then_inc(T.sem.lds, 16)
     g.scalar.dma_start(T.qs[:], T.q[:]).then_inc(T.sem.lds, 16)
     g.vector.memset(T.zero[:], 0.0).then_inc(T.sem.zs, 1)
 
     if sends:
-        slot = T["land%d" % (rank % WB)][:]
-        sem = T.sem["arr%d" % (rank % WB)]
+        s = rank % WB
         total = 0
-        g.wait_ge(T.sem.ldd, 32)
+        loaded = ([(T.sem.ldk, 16)], [(T.sem.ldv, 16)])
         if me["relays"]:
-            busy = set()
-            tr = []
-            for hs, w in _hands(topo, core, me["relays"]):
-                tr.append(_xfer(topo, hs, _pick(topo, core, hs, w, busy), T.sem.rin, T.kvd[:], T.rl[:]))
-                total += w
-            g.remote_dma_fused(tr, local_sem=T.sem.sent)
-        busy = set()
-        tr = []
+            hs = [h for h, p in me["relays"]]
+            total += _send(g, T, topo, core,
+                           [(hs, _hand_width(me["relays"]), (T.kd[:], T.rk[:], T.sem.rink),
+                             (T.vd[:], T.rv[:], T.sem.rinv))], PIPE, loaded)
+            loaded = ([], [])
+        jobs = []
         for part in (me["far"], me["near"]):
             if part:
                 dsts = [cores[r] for r in part]
-                w = _width(topo, core, dsts)
-                tr.append(_xfer(topo, dsts, _pick(topo, core, dsts, w, busy), sem, T.kvd[:], slot))
-                total += w
-        if tr:
-            g.remote_dma_fused(tr, local_sem=T.sem.sent)
+                jobs.append((dsts, _width(topo, core, dsts),
+                             (T.kd[:], T["land%d" % s][:, 0:D], T.sem["ak%d" % s]),
+                             (T.vd[:], T["land%d" % s][:, D:2 * D], T.sem["av%d" % s])))
+        if jobs:
+            total += _send(g, T, topo, core, jobs, False, loaded)
         g.wait_ge(T.sem.sent, total)
 
     early, late = [], []
     for j in range(max(0, rank - WB), rank):
         p = plan[j]
         if rank in p["near"]:
-            early.append((0, j, _width(topo, cores[j], [cores[r] for r in p["near"]])))
+            early.append((0, j, _count(_width(topo, cores[j], [cores[r] for r in p["near"]]), False)))
         elif rank in p["far"]:
-            early.append((1, j, _width(topo, cores[j], [cores[r] for r in p["far"]])))
+            early.append((1, j, _count(_width(topo, cores[j], [cores[r] for r in p["far"]]), False)))
         else:
             for h, part in p["relays"]:
                 if rank in part:
-                    late.append((len(part), j, _width(topo, h, [cores[r] for r in part])))
+                    late.append((len(part), j, _count(_width(topo, h, [cores[r] for r in part]), PIPE)))
     early.sort()
     late.sort()
     groups = [[(None, rank, 0)] + early, late]
@@ -213,7 +232,7 @@ def rank_program(g, core, T, topo):
                 g.tensor.wait_ge(T.sem.lds, 48)
                 kv = T.kvs
             else:
-                g.tensor.wait_ge(T.sem["arr%d" % (j % WB)], w)
+                g.tensor.wait_ge(T.sem["ak%d" % (j % WB)], w)
                 kv = T["land%d" % (j % WB)]
             g.tensor.matmul(T["ps%d" % i][:, 0:QP], kv[:, 0:D], T.qs[:], True, True).then_inc(T.sem["sS%d" % i], 1)
             i += 1
@@ -221,6 +240,8 @@ def rank_program(g, core, T, topo):
         for c, j, w in grp:
             kv = T.kvs if j == rank else T["land%d" % (j % WB)]
             g.tensor.wait_ge(T.sem["sR%d" % i], 1)
+            if j != rank:
+                g.tensor.wait_ge(T.sem["av%d" % (j % WB)], w)
             mm = g.tensor.matmul(T.po[:, 0:QP], kv[:, D:2 * D], T["s%d" % i][:], i == 0, i == n_src - 1)
             if i == n_src - 1:
                 mm.then_inc(T.sem.sO, 1)

from concourse.bass import DstId, RemoteDMATransfer
from concourse.mybir import AluOpType

WB = 4
D = 128
QP = 64
HAND = 4
PIPE = True

SCRATCH = {
    "kd": ("dram", [128, D], "bfloat16"),
    "vd": ("dram", [128, D], "bfloat16"),
    "rk": ("dram", [128, D], "bfloat16"),
    "rv": ("dram", [128, D], "bfloat16"),
    "kvs": ("sbuf", [128, 2 * D], "bfloat16"),
    "qs": ("sbuf", [128, QP], "bfloat16"),
    "land0": ("sbuf", [128, 2 * D], "bfloat16"),
    "land1": ("sbuf", [128, 2 * D], "bfloat16"),
    "land2": ("sbuf", [128, 2 * D], "bfloat16"),
    "land3": ("sbuf", [128, 2 * D], "bfloat16"),
    "zero": ("sbuf", [128, QP], "float32"),
    "s0": ("sbuf", [128, QP], "bfloat16"),
    "s1": ("sbuf", [128, QP], "bfloat16"),
    "s2": ("sbuf", [128, QP], "bfloat16"),
    "s3": ("sbuf", [128, QP], "bfloat16"),
    "s4": ("sbuf", [128, QP], "bfloat16"),
    "ysb": ("sbuf", [128, QP], "bfloat16"),
    "ps0": ("psum", [128, 512], "float32"),
    "ps1": ("psum", [128, 512], "float32"),
    "ps2": ("psum", [128, 512], "float32"),
    "ps3": ("psum", [128, 512], "float32"),
    "ps4": ("psum", [128, 512], "float32"),
    "po": ("psum", [128, 512], "float32"),
}
SEMAPHORES = ["ldk", "ldv", "lds", "rink", "rinv", "sent",
              "ak0", "ak1", "ak2", "ak3", "av0", "av1", "av2", "av3", "zs",
              "sS0", "sS1", "sS2", "sS3", "sS4", "sR0", "sR1", "sR2", "sR3", "sR4", "sO", "sY", "st"]


def _bits(m):
    return [b for b in range(m.bit_length()) if (m >> b) & 1]


def _every(topo):
    return range(topo.CHIPS * topo.CORES_PER_CHIP)


def _pick(topo, src, dsts, n, busy):
    allowed = -1
    for d in dsts:
        allowed &= topo.mask(src, d)
    narrow = -1
    for x in _every(topo):
        if x != src:
            narrow &= topo.mask(src, x)
    free = [b for b in _bits(allowed) if b not in busy]
    order = [b for b in free if not (narrow >> b) & 1] + [b for b in free if (narrow >> b) & 1]
    m = 0
    for b in order[:n]:
        m |= 1 << b
        busy.add(b)
    return m


def _pow2(n, cap):
    p = 1
    while p * 2 <= min(n, cap):
        p *= 2
    return p


def _plan(T, topo):
    cores = list(T.cores)
    n = len(cores)
    group = set(cores)
    taken = set()
    plan = []
    for j, cj in enumerate(cores):
        dests = list(range(j + 1, min(n, j + WB + 1)))
        own = [r for r in dests if topo.may_write(cj, cores[r])]
        near = [r for r in own if topo.chip(cores[r]) == topo.chip(cj)]
        far = [r for r in own if topo.chip(cores[r]) != topo.chip(cj)]
        cross = [r for r in dests if r not in own]
        relays = []
        if cross:
            cand = [h for h in _every(topo)
                    if h not in group and h not in taken
                    and topo.chip(h) == topo.chip(cj) and topo.die(h) == topo.die(cj)
                    and all(topo.may_write(h, cores[r]) for r in cross)]
            k = min(len(cand), len(cross))
            per = -(-len(cross) // k)
            for i in range(k):
                part = cross[i * per:(i + 1) * per]
                if part:
                    relays.append((cand[i], part))
                    taken.add(cand[i])
        plan.append({"near": near, "far": far, "relays": relays})
    return plan


def _width(topo, src, dsts):
    allowed = -1
    for d in dsts:
        allowed &= topo.mask(src, d)
    return _pow2(len(_bits(allowed)), 8)


def _xfer(topo, dsts, mask, sem, src_ap, dst_ap):
    ids = []
    for d in dsts:
        a = topo.addr(d)
        ids.append(DstId(rid=a[0], pnc=a[1]))
    return RemoteDMATransfer(dst_ids=ids, dma_engine_mask=mask, remote_sem=sem,
                             srcs=[src_ap], dsts=[dst_ap] * len(ids), alu_op=0)


def _send(g, T, topo, src, jobs, ahead, waits):
    total = 0
    if ahead:
        masks = []
        busy = set()
        for dsts, w, kk, vv in jobs:
            masks.append(_pick(topo, src, dsts, w, busy))
        for half in (0, 1):
            for sem, val in waits[half]:
                g.wait_ge(sem, val)
            tr = []
            for (dsts, w, kk, vv), m in zip(jobs, masks):
                a = (kk, vv)[half]
                tr.append(_xfer(topo, dsts, m, a[2], a[0], a[1]))
                total += w
            g.remote_dma_fused(tr, local_sem=T.sem.sent)
    else:
        for half in (0, 1):
            for sem, val in waits[half]:
                g.wait_ge(sem, val)
        busy = set()
        tr = []
        for dsts, w, kk, vv in jobs:
            for a in (kk, vv):
                tr.append(_xfer(topo, dsts, _pick(topo, src, dsts, w // 2, busy), a[2], a[0], a[1]))
                total += w // 2
        g.remote_dma_fused(tr, local_sem=T.sem.sent)
    return total


def _count(w, ahead):
    return w if ahead else w // 2


def _hand_width(relays):
    return _pow2(HAND * len(relays), 8)


def _relay_program(g, core, T, topo, j, part, plan):
    cores = list(T.cores)
    dsts = [cores[r] for r in part]
    hw = _count(_hand_width(plan[j]["relays"]), PIPE)
    s = j % WB
    w = _width(topo, core, dsts)
    total = _send(g, T, topo, core,
                  [(dsts, w, (T.rk[:], T["land%d" % s][:, 0:D], T.sem["ak%d" % s]),
                    (T.rv[:], T["land%d" % s][:, D:2 * D], T.sem["av%d" % s]))],
                  PIPE, ([(T.sem.rink, hw)], [(T.sem.rinv, hw)]))
    g.wait_ge(T.sem.sent, total)


def rank_program(g, core, T, topo):
    plan = _plan(T, topo)
    cores = list(T.cores)
    rank = T.rank_of(core)
    if rank is None:
        for j, p in enumerate(plan):
            for h, part in p["relays"]:
                if h == core:
                    _relay_program(g, core, T, topo, j, part, plan)
        return

    me = plan[rank]
    sends = bool(me["near"] or me["far"] or me["relays"])

    if sends:
        g.sync.dma_start(T.kd[:], T.k[:]).then_inc(T.sem.ldk, 16)
        g.scalar.dma_start(T.vd[:], T.v[:]).then_inc(T.sem.ldv, 16)
    g.sync.dma_start(T.kvs[:, 0:D], T.k[:]).then_inc(T.sem.lds, 16)
    g.scalar.dma_start(T.kvs[:, D:2 * D], T.v[:]).then_inc(T.sem.lds, 16)
    g.scalar.dma_start(T.qs[:], T.q[:]).then_inc(T.sem.lds, 16)
    g.vector.memset(T.zero[:], 0.0).then_inc(T.sem.zs, 1)

    if sends:
        s = rank % WB
        total = 0
        loaded = ([(T.sem.ldk, 16)], [(T.sem.ldv, 16)])
        if me["relays"]:
            hs = [h for h, p in me["relays"]]
            total += _send(g, T, topo, core,
                           [(hs, _hand_width(me["relays"]), (T.kd[:], T.rk[:], T.sem.rink),
                             (T.vd[:], T.rv[:], T.sem.rinv))], PIPE, loaded)
            loaded = ([], [])
        jobs = []
        for part in (me["far"], me["near"]):
            if part:
                dsts = [cores[r] for r in part]
                jobs.append((dsts, _width(topo, core, dsts),
                             (T.kd[:], T["land%d" % s][:, 0:D], T.sem["ak%d" % s]),
                             (T.vd[:], T["land%d" % s][:, D:2 * D], T.sem["av%d" % s])))
        if jobs:
            total += _send(g, T, topo, core, jobs, False, loaded)
        g.wait_ge(T.sem.sent, total)

    early, late = [], []
    for j in range(max(0, rank - WB), rank):
        p = plan[j]
        if rank in p["near"]:
            early.append((0, j, _count(_width(topo, cores[j], [cores[r] for r in p["near"]]), False)))
        elif rank in p["far"]:
            early.append((1, j, _count(_width(topo, cores[j], [cores[r] for r in p["far"]]), False)))
        else:
            for h, part in p["relays"]:
                if rank in part:
                    late.append((len(part), j, _count(_width(topo, h, [cores[r] for r in part]), PIPE)))
    early.sort()
    late.sort()
    groups = [[(None, rank, 0)] + early, late]
    n_src = 1 + len(early) + len(late)

    i = 0
    for grp in groups:
        first = i
        for c, j, w in grp:
            if j == rank:
                g.tensor.wait_ge(T.sem.lds, 48)
                kv = T.kvs
            else:
                g.tensor.wait_ge(T.sem["ak%d" % (j % WB)], w)
                kv = T["land%d" % (j % WB)]
            g.tensor.matmul(T["ps%d" % i][:, 0:QP], kv[:, 0:D], T.qs[:], True, True).then_inc(T.sem["sS%d" % i], 1)
            i += 1
        i = first
        for c, j, w in grp:
            kv = T.kvs if j == rank else T["land%d" % (j % WB)]
            g.tensor.wait_ge(T.sem["sR%d" % i], 1)
            if j != rank:
                g.tensor.wait_ge(T.sem["av%d" % (j % WB)], w)
            mm = g.tensor.matmul(T.po[:, 0:QP], kv[:, D:2 * D], T["s%d" % i][:], i == 0, i == n_src - 1)
            if i == n_src - 1:
                mm.then_inc(T.sem.sO, 1)
            i += 1

    g.vector.wait_ge(T.sem.zs, 1)
    for i in range(n_src):
        g.vector.wait_ge(T.sem["sS%d" % i], 1)
        g.vector.tensor_tensor(T["s%d" % i][:], T["ps%d" % i][:, 0:QP], T.zero[:], AluOpType.max).then_inc(
            T.sem["sR%d" % i], 1)
    g.vector.wait_ge(T.sem.sO, 1)
    g.vector.tensor_copy(T.ysb[:], T.po[:, 0:QP]).then_inc(T.sem.sY, 1)

    g.sync.wait_ge(T.sem.sY, 1)
    g.sync.dma_start(T.y[:], T.ysb[:]).then_inc(T.sem.st, 16)
    g.sync.wait_ge(T.sem.st, 16)
